import numpy as np
import ml_dtypes


def mxq(x, axis, fmt="e4m3"):
    dtype, down = {"e4m3": (ml_dtypes.float8_e4m3fn, 7), "e5m2": (ml_dtypes.float8_e5m2, 14)}[fmt]
    v = np.moveaxis(np.asarray(x, np.float32).astype(ml_dtypes.bfloat16).astype(np.float64), axis, -1)
    blocks = v.reshape(v.shape[:-1] + (-1, 32))
    amax = np.abs(blocks).max(-1, keepdims=True)
    byte = np.maximum(np.where(amax > 0, np.frexp(amax)[1] - 1 + 127, 0) - down, 1)
    scale = np.exp2(byte - 127.0)
    codes = (blocks / scale).astype(np.float32).astype(dtype).astype(np.float64)
    return np.moveaxis((codes * scale).reshape(v.shape), -1, axis)


WIDE = False


def mx_kscale(k):
    if not WIDE:
        return np.ones(k)
    levels = np.array([10, -10, 5, -5, 0])
    if k % 512:
        return np.exp2(np.random.permutation(np.resize(levels, k // 32))).repeat(32)
    a = np.empty((k // 512, 16))
    for p in range(k // 512):
        a[p, :8] = np.random.permutation(np.resize(levels, 8))
        for g in range(8):
            far = levels[np.abs(levels - a[p, g]) >= 10]
            a[p, g + 8] = far[np.random.randint(len(far))]
    return np.exp2(a.ravel()).repeat(32)


def f64(x):
    return np.asarray(x).astype(np.float64)


def striped(idx):
    return np.tile(idx.reshape(-1, 16).T, (8, 1)).astype(np.uint16)


def unstriped(offs):
    return offs[:16].T.reshape(-1).astype(np.int64)


def striped8(idx):
    return np.concatenate([x.reshape(-1, 16).T for x in idx]).astype(np.uint16)


def runs(offs, k):
    lists = np.stack([offs[16 * r : 16 * r + 16].T.reshape(-1) for r in range(8)]).astype(np.int64)
    return lists[np.arange(k) % 512 // 64]


def pack_weight(w):
    k, n = w.shape
    w = f64(np.asarray(w, np.float32).astype(ml_dtypes.bfloat16)).reshape(k // 32, 32, n)
    amax = np.abs(w).max(1)
    byte = np.clip(np.where(amax > 0, np.frexp(amax)[1] - 1 + 127 - 7, 1), 1, 254)
    scaled = (w * np.exp2(127.0 - byte)[:, None, :]).reshape(k, n).astype(np.float32)
    words = np.ascontiguousarray(scaled.reshape(k // 512, 128, 4, n).transpose(0, 1, 3, 2)).astype(ml_dtypes.float8_e4m3fn).view(np.uint8)
    return words, np.ascontiguousarray(byte.astype(np.uint8).reshape(k // 512, 16, n))


def unpack_weight(words, scales):
    g, p, n, _ = words.shape
    vals = np.ascontiguousarray(words).view(ml_dtypes.float8_e4m3fn).astype(np.float64) * np.repeat(np.exp2(scales.astype(np.float64) - 127.0), 8, axis=1)[..., None]
    return vals.transpose(0, 1, 3, 2).reshape(g * 512, n)


K, T, S, N, H, W = 512, 2048, 256, 512, 512, 1024


def setup_inputs():
    n = np.random.standard_normal
    s = mx_kscale(K)[:, None]
    u = mx_kscale(H)
    packed_xT = pack_weight(n((K, T)) * s)
    return {
        "x_words": packed_xT[0],
        "x_scales": packed_xT[1],
        "w1": (n((K, H)) / np.sqrt(K) / s).astype(np.float32),
        "w2": (n((K, H)) / np.sqrt(K) / s).astype(np.float32),
        "gn": (np.random.uniform(0.5, 1.5, (H, 1)) * u[:, None]).astype(np.float32),
        "gm": (np.random.uniform(0.5, 1.5, (H, 1)) * u[:, None]).astype(np.float32),
        "w3": (n((H, N)) / np.sqrt(2 * H) / u[:, None]).astype(np.float32),
        "w4": (n((H, N)) / np.sqrt(2 * H) / u[:, None]).astype(np.float32),
        "offs": striped(np.random.permutation(T)[:S]),
        "hz": striped8(np.random.randint(0, T, (8, S))),
        "n1": striped(np.random.randint(0, S, W)),
        "n2": striped8(np.stack([np.random.permutation(S) for _ in range(8)])),
        "n3": striped8(np.stack([np.random.permutation(S) for _ in range(8)])),
        "n4": striped(np.random.permutation(S)),
        "n5": striped(np.random.permutation(S)),
    }


def reference(x_words, x_scales, w1, w2, gn, gm, w3, w4, offs, hz, n1, n2, n3, n4, n5):
    xq = unpack_weight(x_words, x_scales)[:, unstriped(offs)]
    y = mxq(f64(w1), 0, "e4m3").T @ xq
    mb = y[:, unstriped(n1)]
    mn = mb.reshape(H, S, 4).min(axis=2)
    mx = mb.reshape(H, S, 4).max(axis=2)
    z = f64(gn) * (np.maximum(y, mn) - (0.5 * mx))
    x_hz = unpack_weight(x_words, x_scales)[np.arange(K)[:, None], runs(hz, K)]
    d = mxq(f64(w2), 0, "e4m3").T @ x_hz
    z2 = f64(gm) * ((d * (d[np.arange(H)[:, None], runs(n2, H)])) * (np.tanh(d[np.arange(H)[:, None], runs(n3, H)])))
    h = mxq(f64(w3), 0, "e4m3").T @ mxq(z, 0, "e4m3") + mxq(f64(w4), 0, "e4m3").T @ mxq(z2, 0, "e4m3")
    st = np.maximum(h, h[:, unstriped(n4)])
    return st[:, unstriped(n5)] - (0.5 * h)

@@ -1,0 +1,219 @@
+from contextlib import ExitStack
+
+import concourse.mybir as mybir
+
+K, T, S, N, H, W = 512, 2048, 256, 512, 512, 1024
+FLOPS = 2 * S * (K * H + K * H + H * N + H * N)
+
+F32 = mybir.dt.float32
+BF16 = mybir.dt.bfloat16
+I32 = mybir.dt.int32
+U32 = mybir.dt.uint32
+U16 = mybir.dt.uint16
+U8 = mybir.dt.uint8
+FP8X4 = mybir.dt.float8_e4m3fn_x4
+ALU = mybir.AluOpType
+ACT = mybir.ActivationFunctionType
+
+P = 128
+PACK = 4
+HALF = S // 2
+Y_WINDOW = W + 16
+
+
+def tile_picked_hjoingmidcubehopb_none_p_kernel(
+    tc, x_words, x_scales, w1, w2, gn, gm, w3, w4, offs, hz, n1, n2, n3, n4, n5, out
+):
+    nc = tc.nc
+    with ExitStack() as ctx:
+        keep = ctx.enter_context(tc.tile_pool(name="keep", bufs=1))
+        psum = ctx.enter_context(tc.psum_pool(name="psum", bufs=1))
+
+        def sb(name, shape, dtype):
+            return keep.tile(shape, dtype, name=name, align_bytes=64)
+
+        def load_list(name, src):
+            tile = keep.tile(list(src.shape), U16, name=name)
+            nc.sync.dma_start(tile[:], src)
+            return tile
+
+        def load_weight(name, src):
+            raw = sb(name, [P, PACK, 512], F32)
+            nc.sync.dma_start(raw[:], src.rearrange("(p j) c -> p j c", j=PACK))
+            return raw
+
+        def half(lst, u):
+            return lst[:, 8 * u : 8 * u + 8]
+
+        xs = sb("xs", [P, T], U8)
+        nc.vector.memset(xs[:].bitcast(I32), 0)
+        hz_plane = sb("hz_plane", [P, S], U8)
+        nc.gpsimd.memset(hz_plane[:].bitcast(I32), 0)
+        y_win = [sb("y_win%d" % t, [P, Y_WINDOW], F32) for t in range(PACK)]
+        for t in range(PACK):
+            nc.vector.memset(y_win[t][:, S:], 0.0)
+
+        offs_t = load_list("offs_t", offs)
+        hz_t = load_list("hz_t", hz)
+        w1_raw = load_weight("w1_raw", w1)
+        rows = x_scales[0].bitcast(I32)
+        nc.sync.dma_start(xs[0:P:8, :].bitcast(I32), rows)
+        for r in range(1, 4):
+            nc.sync.dma_start(xs[r:P:32, :].bitcast(I32), rows[r:16:4, :])
+        xw = sb("xw", [P, T], I32)
+        nc.sync.dma_start(xw[:], x_words[0].rearrange("p n t -> p (n t)").bitcast(I32))
+        n1_t = load_list("n1_t", n1)
+        w2_raw = load_weight("w2_raw", w2)
+        n2_t = load_list("n2_t", n2)
+        n3_t = load_list("n3_t", n3)
+        w3_raw = load_weight("w3_raw", w3)
+        w4_raw = load_weight("w4_raw", w4)
+        n4_t = load_list("n4_t", n4)
+        n5_t = load_list("n5_t", n5)
+        gn_t = sb("gn_t", [P, PACK], F32)
+        gm_t = sb("gm_t", [P, PACK], F32)
+        nc.gpsimd.dma_start(gn_t[:], gn.rearrange("(p t) o -> p (t o)", t=PACK))
+        nc.gpsimd.dma_start(gm_t[:], gm.rearrange("(p t) o -> p (t o)", t=PACK))
+
+        def cast_dealt(copy, grouped, raw, m0, m1):
+            dst = grouped[:].rearrange("p (t m j) -> p m j t", t=PACK, j=PACK)
+            src = raw[:].rearrange("p j (m t) -> p m j t", t=PACK)
+            copy(dst[:, m0:m1], src[:, m0:m1])
+
+        def cast_plain(copy, grouped, raw, c0, c1):
+            dst = grouped[:].rearrange("p (c i j) -> p c j i", i=4, j=PACK)
+            src = raw[:].rearrange("p j (c i) -> p c j i", i=4)
+            copy(dst[:, c0:c1], src[:, c0:c1])
+
+        def quantize(name, grouped, width):
+            codes = sb(name + "_codes", [P, width], U32)
+            plane = sb(name + "_plane", [P, width], U8)
+            nc.vector.quantize_mx(out=codes[:].bitcast(FP8X4), scales=plane[:], in_=grouped)
+            return codes, plane
+
+        def product(acc, lhs, cols, rhs, start, stop):
+            nc.tensor.matmul_mx(
+                out=acc, lhsT=lhs[0][:, cols].bitcast(FP8X4), lhsT_scale=lhs[1][:, cols],
+                rhs=rhs[0].bitcast(FP8X4), rhs_scale=rhs[1], start=start, stop=stop,
+            )
+
+        w1_g = sb("w1_g", [P, 2048], BF16)
+        cast_dealt(nc.vector.tensor_copy, w1_g, w1_raw, 0, 64)
+        cast_dealt(nc.scalar.copy, w1_g, w1_raw, 64, 128)
+        offs_plane = sb("offs_plane", [P, S], U8)
+        nc.vector.tensor_copy(offs_plane[:], xs[:].indirect(offs_t[:]))
+        w1_q = quantize("w1", w1_g[:], 512)
+        offs_words = sb("offs_words", [P, S], U32)
+        nc.vector.tensor_copy(offs_words[:], xw[:].bitcast(U32).indirect(offs_t[:]))
+        y_ps = [psum.tile([P, S], F32, name="y_ps%d" % t, tag="yh%d" % t) for t in range(PACK)]
+        for t in range(PACK):
+            product(y_ps[t][:], w1_q, slice(P * t, P * (t + 1)), (offs_words[:], offs_plane[:]), True, True)
+        members = [sb("members%d" % t, [P, W], F32) for t in range(PACK)]
+        for t in range(PACK):
+            nc.scalar.copy(y_win[t][:, :S], y_ps[t][:])
+        for t in range(PACK):
+            nc.scalar.activation(members[t][:], y_win[t][:].indirect(n1_t[:]), ACT.Copy)
+
+        hz_bytes = sb("hz_bytes", [P, S], U8)
+        nc.vector.tensor_copy(hz_bytes[:], xs[:].indirect(hz_t[:]))
+        for r, src in enumerate((0, 1, 16, 24)):
+            nc.scalar.dma_start(hz_plane[r:P:32, :].bitcast(I32), hz_bytes[src:P:32, :].bitcast(I32))
+        hz_words = sb("hz_words", [P, S], U32)
+        nc.vector.tensor_copy(hz_words[:], xw[:].bitcast(U32).indirect(hz_t[:]))
+        w2_g = sb("w2_g", [P, 2048], BF16)
+        cast_dealt(nc.vector.tensor_copy, w2_g, w2_raw, 0, 128)
+        w2_q = quantize("w2", w2_g[:], 512)
+        d_ps = [psum.tile([P, S], F32, name="d_ps%d" % t, tag="d%d" % t) for t in range(PACK)]
+        for t in range(PACK):
+            product(d_ps[t][:], w2_q, slice(P * t, P * (t + 1)), (hz_words[:], hz_plane[:]), True, True)
+        gd_win = [sb("gd_win%d" % t, [P, S], F32) for t in range(PACK)]
+        th_win = [sb("th_win%d" % t, [P, S], F32) for t in range(PACK)]
+        for t in range(PACK):
+            nc.scalar.activation(gd_win[t][:], d_ps[t][:], ACT.Copy, scale=gm_t[:, t : t + 1])
+            nc.scalar.activation(th_win[t][:], d_ps[t][:], ACT.Tanh)
+        gd_got = sb("gd_got", [P, PACK, S], F32)
+        th_got = sb("th_got", [P, PACK, S], F32)
+        for t in range(PACK):
+            for u in range(2):
+                nc.scalar.activation(
+                    gd_got[:, t, HALF * u : HALF * (u + 1)], gd_win[t][:].indirect(half(n2_t, u)), ACT.Copy
+                )
+        for u in range(2):
+            for t in range(PACK):
+                nc.scalar.activation(
+                    th_got[:, t, HALF * u : HALF * (u + 1)], th_win[t][:].indirect(half(n3_t, u)), ACT.Copy
+                )
+
+        b_all = sb("b_all", [P, PACK, S], F32)
+
+        def combine(t):
+            g = members[t][:].rearrange("p (j u e) -> p j u e", u=2, e=2)
+            lo = sb("lo%d" % t, [P, S, 2], F32)
+            hi = sb("hi%d" % t, [P, S, 2], F32)
+            mn = sb("mn%d" % t, [P, S], F32)
+            mx = sb("mx%d" % t, [P, S], F32)
+            a = sb("a%d" % t, [P, S], F32)
+            nc.vector.tensor_tensor(lo[:], g[:, :, 0, :], g[:, :, 1, :], ALU.min)
+            nc.vector.tensor_tensor(hi[:], g[:, :, 0, :], g[:, :, 1, :], ALU.max)
+            nc.vector.tensor_tensor(mn[:], lo[:, :, 0], lo[:, :, 1], ALU.min)
+            nc.vector.tensor_tensor(mx[:], hi[:, :, 0], hi[:, :, 1], ALU.max)
+            nc.vector.tensor_tensor(a[:], y_ps[t][:], mn[:], ALU.max)
+            nc.vector.scalar_tensor_tensor(b_all[:, t, :], mx[:], -0.5, a[:], ALU.mult, ALU.add)
+
+        combine(0)
+        w3_g = sb("w3_g", [P, 2048], BF16)
+        cast_plain(nc.vector.tensor_copy, w3_g, w3_raw, 0, 128)
+        w3_q = quantize("w3", w3_g[:], 512)
+        combine(1)
+        w4_g = sb("w4_g", [P, 2048], BF16)
+        cast_plain(nc.vector.tensor_copy, w4_g, w4_raw, 0, 128)
+        w4_q = quantize("w4", w4_g[:], 512)
+        combine(2)
+        combine(3)
+
+        def woven(ap):
+            return ap.rearrange("p t (c i) -> p c t i", i=4)
+
+        z_g = sb("z_g", [P, S * PACK], BF16)
+        nc.vector.tensor_tensor(
+            z_g[:].rearrange("p (c i t) -> p c t i", i=4, t=PACK),
+            woven(b_all[:]),
+            gn_t[:].unsqueeze(1).unsqueeze(3).broadcast_to([P, S // 4, PACK, 4]),
+            ALU.mult,
+        )
+        z_codes, z_plane = quantize("z", z_g[:], S)
+        h_ps = [psum.tile([P, S], F32, name="h_ps%d" % m, tag="yh%d" % m) for m in range(PACK)]
+        for m in range(PACK):
+            product(h_ps[m][:], w3_q, slice(P * m, P * (m + 1)), (z_codes[:], z_plane[:]), True, False)
+
+        pair = sb("pair", [P, PACK, S], F32)
+        for t in range(PACK):
+            nc.vector.tensor_tensor(pair[:, t, :], d_ps[t][:], gd_got[:, t, :], ALU.mult)
+        z2_g = sb("z2_g", [P, S * PACK], BF16)
+        z2_codes = sb("z2_codes", [P, S], U32)
+        z2_plane = sb("z2_plane", [P, S], U8)
+        for u in range(2):
+            cols = slice(HALF * u, HALF * (u + 1))
+            part = z2_g[:, PACK * HALF * u : PACK * HALF * (u + 1)]
+            nc.vector.tensor_tensor(
+                part.rearrange("p (c i t) -> p c t i", i=4, t=PACK),
+                woven(pair[:, :, cols]), woven(th_got[:, :, cols]), ALU.mult,
+            )
+            nc.vector.quantize_mx(out=z2_codes[:, cols].bitcast(FP8X4), scales=z2_plane[:, cols], in_=part)
+        for m in range(PACK):
+            product(h_ps[m][:], w4_q, slice(P * m, P * (m + 1)), (z2_codes[:], z2_plane[:]), False, True)
+
+        for m in range(PACK):
+            h_win = sb("h_win%d" % m, [P, S], F32)
+            h_got = sb("h_got%d" % m, [P, S], F32)
+            st_win = sb("st_win%d" % m, [P, S], F32)
+            st_got = sb("st_got%d" % m, [P, S], F32)
+            res = sb("res%d" % m, [P, S], F32)
+            nc.scalar.copy(h_win[:], h_ps[m][:])
+            for u in range(2):
+                nc.vector.tensor_copy(h_got[:, HALF * u : HALF * (u + 1)], h_win[:].indirect(half(n4_t, u)))
+            nc.vector.tensor_tensor(st_win[:], h_win[:], h_got[:], ALU.max)
+            for u in range(2):
+                nc.scalar.activation(st_got[:, HALF * u : HALF * (u + 1)], st_win[:].indirect(half(n5_t, u)), ACT.Copy)
+            nc.vector.scalar_tensor_tensor(res[:], h_win[:], -0.5, st_got[:], ALU.mult, ALU.add)
+            nc.sync.dma_start(out[P * m : P * (m + 1), :], res[:])

@@ -18,7 +18,16 @@ ACT = mybir.ActivationFunctionType
 P = 128
 PACK = 4
 HALF = S // 2
+HALVES = ((0, HALF), (HALF, S))
+
 Y_WINDOW = W + 16
+GD_WINDOW = 2 * S
+H_WINDOW = S + HALF
+ST_WINDOW = S + 16
+
+W1_ON_VECTOR = 80
+EARLY_BLOCKS = 2
+N4_ON_SCALAR = 2
 
 
 def tile_picked_hjoingmidcubehopb_none_p_kernel(
@@ -29,8 +38,8 @@ def tile_picked_hjoingmidcubehopb_none_p_kernel(
         keep = ctx.enter_context(tc.tile_pool(name="keep", bufs=1))
         psum = ctx.enter_context(tc.psum_pool(name="psum", bufs=1))
 
-        def sb(name, shape, dtype):
-            return keep.tile(shape, dtype, name=name, align_bytes=64)
+        def sb(name, shape, dtype, reuse=None):
+            return keep.tile(shape, dtype, name=name, tag=reuse or name, align_bytes=64)
 
         def load_list(name, src):
             tile = keep.tile(list(src.shape), U16, name=name)
@@ -38,182 +47,201 @@ def tile_picked_hjoingmidcubehopb_none_p_kernel(
             return tile
 
         def load_weight(name, src):
-            raw = sb(name, [P, PACK, 512], F32)
+            raw = sb(name, [P, PACK, src.shape[1]], F32)
             nc.sync.dma_start(raw[:], src.rearrange("(p j) c -> p j c", j=PACK))
             return raw
 
-        def half(lst, u):
-            return lst[:, 8 * u : 8 * u + 8]
+        def load_gain(name, src):
+            tile = sb(name, [P, PACK], F32)
+            nc.sync.dma_start(tile[:], src.rearrange("(p t) o -> p (t o)", t=PACK))
+            return tile
 
-        xs = sb("xs", [P, T], U8)
-        nc.vector.memset(xs[:].bitcast(I32), 0)
+        def entries(lst, c0, c1):
+            return lst[:, c0 // 16 : c1 // 16]
+
+        def round_dealt(copy, rounded, raw, m0, m1):
+            dst = rounded[:].rearrange("p (t m j) -> p m j t", t=PACK, j=PACK)
+            src = raw[:].rearrange("p j (m t) -> p m j t", t=PACK)
+            copy(dst[:, m0:m1], src[:, m0:m1])
+
+        def round_plain(copy, rounded, raw, c0, c1):
+            dst = rounded[:].rearrange("p (c i j) -> p c j i", i=4, j=PACK)
+            copy(dst, raw[:, :, c0:c1].rearrange("p j (c i) -> p c j i", i=4))
+
+        def quantize(name, rounded, reuse=None):
+            width = rounded.shape[1] // PACK
+            words = sb(name + "_words", [P, width], U32, reuse)
+            plane = sb(name + "_plane", [P, width], U8)
+            nc.vector.quantize_mx(out=words[:].bitcast(FP8X4), scales=plane[:], in_=rounded[:])
+            return words, plane
+
+        def product(acc, weight, block, moving, start, stop):
+            cols = slice(P * block, P * (block + 1))
+            nc.tensor.matmul_mx(
+                out=acc[:],
+                lhsT=weight[0][:, cols].bitcast(FP8X4),
+                lhsT_scale=weight[1][:, cols],
+                rhs=moving[0][:].bitcast(FP8X4),
+                rhs_scale=moving[1][:],
+                start=start,
+                stop=stop,
+            )
+
+        def by_pairs(planes):
+            return planes.rearrange("p t (c i) -> p c t i", i=2)
+
+        def woven(rounded):
+            return rounded.rearrange("p (c i t) -> p c t i", i=2, t=PACK)
+
+        x_bytes = sb("x_bytes", [P, T], U8)
+        nc.gpsimd.memset(x_bytes[:].bitcast(I32), 0)
         hz_plane = sb("hz_plane", [P, S], U8)
         nc.gpsimd.memset(hz_plane[:].bitcast(I32), 0)
         y_win = [sb("y_win%d" % t, [P, Y_WINDOW], F32) for t in range(PACK)]
-        for t in range(PACK):
-            nc.vector.memset(y_win[t][:, S:], 0.0)
+        for win in y_win:
+            nc.vector.memset(win[:, S:], 0.0)
+        gd_win = [sb("gd_win%d" % t, [P, GD_WINDOW], F32) for t in range(PACK)]
+        h_win = [sb("h_win%d" % m, [P, H_WINDOW], F32) for m in range(PACK)]
+        st_win = [sb("st_win%d" % m, [P, ST_WINDOW], F32) for m in range(PACK)]
+        for win in gd_win + h_win + st_win:
+            nc.gpsimd.memset(win[:, S:], 0.0)
 
         offs_t = load_list("offs_t", offs)
         hz_t = load_list("hz_t", hz)
         w1_raw = load_weight("w1_raw", w1)
-        rows = x_scales[0].bitcast(I32)
-        nc.sync.dma_start(xs[0:P:8, :].bitcast(I32), rows)
-        for r in range(1, 4):
-            nc.sync.dma_start(xs[r:P:32, :].bitcast(I32), rows[r:16:4, :])
-        xw = sb("xw", [P, T], I32)
-        nc.sync.dma_start(xw[:], x_words[0].rearrange("p n t -> p (n t)").bitcast(I32))
+        x_tile = sb("x_tile", [P, T], I32)
+        nc.sync.dma_start(x_tile[:], x_words[0].rearrange("p n j -> p (n j)").bitcast(I32))
         n1_t = load_list("n1_t", n1)
+        scale_rows = x_scales[0].bitcast(I32)
+        nc.sync.dma_start(x_bytes[0:P:8, :].bitcast(I32), scale_rows)
+        for r in range(1, 4):
+            nc.sync.dma_start(x_bytes[r:P:32, :].bitcast(I32), scale_rows[r:16:4, :])
         w2_raw = load_weight("w2_raw", w2)
-        n2_t = load_list("n2_t", n2)
-        n3_t = load_list("n3_t", n3)
         w3_raw = load_weight("w3_raw", w3)
         w4_raw = load_weight("w4_raw", w4)
+        gm_t = load_gain("gm_t", gm)
+        gn_t = load_gain("gn_t", gn)
+        n2_t = load_list("n2_t", n2)
+        n3_t = load_list("n3_t", n3)
         n4_t = load_list("n4_t", n4)
         n5_t = load_list("n5_t", n5)
-        gn_t = sb("gn_t", [P, PACK], F32)
-        gm_t = sb("gm_t", [P, PACK], F32)
-        nc.gpsimd.dma_start(gn_t[:], gn.rearrange("(p t) o -> p (t o)", t=PACK))
-        nc.gpsimd.dma_start(gm_t[:], gm.rearrange("(p t) o -> p (t o)", t=PACK))
 
-        def cast_dealt(copy, grouped, raw, m0, m1):
-            dst = grouped[:].rearrange("p (t m j) -> p m j t", t=PACK, j=PACK)
-            src = raw[:].rearrange("p j (m t) -> p m j t", t=PACK)
-            copy(dst[:, m0:m1], src[:, m0:m1])
-
-        def cast_plain(copy, grouped, raw, c0, c1):
-            dst = grouped[:].rearrange("p (c i j) -> p c j i", i=4, j=PACK)
-            src = raw[:].rearrange("p j (c i) -> p c j i", i=4)
-            copy(dst[:, c0:c1], src[:, c0:c1])
-
-        def quantize(name, grouped, width):
-            codes = sb(name + "_codes", [P, width], U32)
-            plane = sb(name + "_plane", [P, width], U8)
-            nc.vector.quantize_mx(out=codes[:].bitcast(FP8X4), scales=plane[:], in_=grouped)
-            return codes, plane
-
-        def product(acc, lhs, cols, rhs, start, stop):
-            nc.tensor.matmul_mx(
-                out=acc, lhsT=lhs[0][:, cols].bitcast(FP8X4), lhsT_scale=lhs[1][:, cols],
-                rhs=rhs[0].bitcast(FP8X4), rhs_scale=rhs[1], start=start, stop=stop,
-            )
-
-        w1_g = sb("w1_g", [P, 2048], BF16)
-        cast_dealt(nc.vector.tensor_copy, w1_g, w1_raw, 0, 64)
-        cast_dealt(nc.scalar.copy, w1_g, w1_raw, 64, 128)
+        w1_rounded = sb("w1_rounded", [P, PACK * H], BF16)
+        round_dealt(nc.vector.tensor_copy, w1_rounded, w1_raw, 0, W1_ON_VECTOR)
+        round_dealt(nc.scalar.copy, w1_rounded, w1_raw, W1_ON_VECTOR, P)
         offs_plane = sb("offs_plane", [P, S], U8)
-        nc.vector.tensor_copy(offs_plane[:], xs[:].indirect(offs_t[:]))
-        w1_q = quantize("w1", w1_g[:], 512)
+        nc.vector.tensor_copy(offs_plane[:], x_bytes[:].indirect(offs_t[:]))
+        w1_mx = quantize("w1", w1_rounded)
         offs_words = sb("offs_words", [P, S], U32)
-        nc.vector.tensor_copy(offs_words[:], xw[:].bitcast(U32).indirect(offs_t[:]))
+        nc.vector.tensor_copy(offs_words[:], x_tile[:].bitcast(U32).indirect(offs_t[:]))
         y_ps = [psum.tile([P, S], F32, name="y_ps%d" % t, tag="yh%d" % t) for t in range(PACK)]
         for t in range(PACK):
-            product(y_ps[t][:], w1_q, slice(P * t, P * (t + 1)), (offs_words[:], offs_plane[:]), True, True)
+            product(y_ps[t], w1_mx, t, (offs_words, offs_plane), True, True)
         members = [sb("members%d" % t, [P, W], F32) for t in range(PACK)]
+        nc.scalar.copy(y_win[0][:, :S], y_ps[0][:])
         for t in range(PACK):
-            nc.scalar.copy(y_win[t][:, :S], y_ps[t][:])
-        for t in range(PACK):
+            if t + 1 < PACK:
+                nc.scalar.copy(y_win[t + 1][:, :S], y_ps[t + 1][:])
             nc.scalar.activation(members[t][:], y_win[t][:].indirect(n1_t[:]), ACT.Copy)
 
         hz_bytes = sb("hz_bytes", [P, S], U8)
-        nc.vector.tensor_copy(hz_bytes[:], xs[:].indirect(hz_t[:]))
-        for r, src in enumerate((0, 1, 16, 24)):
-            nc.scalar.dma_start(hz_plane[r:P:32, :].bitcast(I32), hz_bytes[src:P:32, :].bitcast(I32))
+        nc.vector.tensor_copy(hz_bytes[:], x_bytes[:].indirect(hz_t[:]))
+        for r in range(4):
+            nc.sync.dma_start(hz_plane[r:P:32, :].bitcast(I32), hz_bytes[8 * r : P : 32, :].bitcast(I32))
         hz_words = sb("hz_words", [P, S], U32)
-        nc.vector.tensor_copy(hz_words[:], xw[:].bitcast(U32).indirect(hz_t[:]))
-        w2_g = sb("w2_g", [P, 2048], BF16)
-        cast_dealt(nc.vector.tensor_copy, w2_g, w2_raw, 0, 128)
-        w2_q = quantize("w2", w2_g[:], 512)
+        nc.vector.tensor_copy(hz_words[:], x_tile[:].bitcast(U32).indirect(hz_t[:]))
+        w2_rounded = sb("w2_rounded", [P, PACK * H], BF16)
+        round_dealt(nc.vector.tensor_copy, w2_rounded, w2_raw, 0, P)
+        w2_mx = quantize("w2", w2_rounded)
         d_ps = [psum.tile([P, S], F32, name="d_ps%d" % t, tag="d%d" % t) for t in range(PACK)]
         for t in range(PACK):
-            product(d_ps[t][:], w2_q, slice(P * t, P * (t + 1)), (hz_words[:], hz_plane[:]), True, True)
-        gd_win = [sb("gd_win%d" % t, [P, S], F32) for t in range(PACK)]
+            product(d_ps[t], w2_mx, t, (hz_words, hz_plane), True, True)
+
+        upper = sb("upper", [P, PACK, S], F32)
+        mx = sb("mx", [P, PACK, S], F32)
+
+        def extremes(t):
+            four = members[t][:].rearrange("p (j u e) -> p j u e", u=2, e=2)
+            left = sb("left%d" % t, [P, 2, S, 2], F32, reuse="w3_raw")
+            low, high = left[:, 0], left[:, 1]
+            mn = sb("mn%d" % t, [P, S], F32)
+            nc.vector.tensor_tensor(low, four[:, :, 0, :], four[:, :, 1, :], ALU.min)
+            nc.vector.tensor_tensor(high, four[:, :, 0, :], four[:, :, 1, :], ALU.max)
+            nc.vector.tensor_tensor(mn[:], low[:, :, 0], low[:, :, 1], ALU.min)
+            nc.vector.tensor_tensor(mx[:, t, :], high[:, :, 0], high[:, :, 1], ALU.max)
+            nc.vector.tensor_tensor(upper[:, t, :], y_ps[t][:], mn[:], ALU.max)
+
+        w3_rounded = sb("w3_rounded", [P, PACK * N], BF16)
+        round_plain(nc.vector.tensor_copy, w3_rounded, w3_raw, 0, N)
+        extremes(0)
+        w3_mx = quantize("w3", w3_rounded)
+        extremes(1)
+
         th_win = [sb("th_win%d" % t, [P, S], F32) for t in range(PACK)]
         for t in range(PACK):
-            nc.scalar.activation(gd_win[t][:], d_ps[t][:], ACT.Copy, scale=gm_t[:, t : t + 1])
+            nc.scalar.activation(gd_win[t][:, :S], d_ps[t][:], ACT.Copy, scale=gm_t[:, t : t + 1])
             nc.scalar.activation(th_win[t][:], d_ps[t][:], ACT.Tanh)
         gd_got = sb("gd_got", [P, PACK, S], F32)
         th_got = sb("th_got", [P, PACK, S], F32)
         for t in range(PACK):
-            for u in range(2):
-                nc.scalar.activation(
-                    gd_got[:, t, HALF * u : HALF * (u + 1)], gd_win[t][:].indirect(half(n2_t, u)), ACT.Copy
-                )
-        for u in range(2):
+            nc.scalar.activation(gd_got[:, t, :], gd_win[t][:].indirect(n2_t[:]), ACT.Copy)
+        for c0, c1 in HALVES:
             for t in range(PACK):
-                nc.scalar.activation(
-                    th_got[:, t, HALF * u : HALF * (u + 1)], th_win[t][:].indirect(half(n3_t, u)), ACT.Copy
-                )
+                nc.scalar.activation(th_got[:, t, c0:c1], th_win[t][:].indirect(entries(n3_t, c0, c1)), ACT.Copy)
 
-        b_all = sb("b_all", [P, PACK, S], F32)
+        early_columns = P * EARLY_BLOCKS
+        w4_early_rounded = sb("w4_early_rounded", [P, PACK * early_columns], BF16)
+        round_plain(nc.vector.tensor_copy, w4_early_rounded, w4_raw, 0, early_columns)
+        w4_late_rounded = sb("w4_late_rounded", [P, PACK * (N - early_columns)], BF16, reuse="th_win%d" % (PACK - 1))
+        round_plain(nc.scalar.copy, w4_late_rounded, w4_raw, early_columns, N)
+        extremes(2)
+        extremes(3)
 
-        def combine(t):
-            g = members[t][:].rearrange("p (j u e) -> p j u e", u=2, e=2)
-            lo = sb("lo%d" % t, [P, S, 2], F32)
-            hi = sb("hi%d" % t, [P, S, 2], F32)
-            mn = sb("mn%d" % t, [P, S], F32)
-            mx = sb("mx%d" % t, [P, S], F32)
-            a = sb("a%d" % t, [P, S], F32)
-            nc.vector.tensor_tensor(lo[:], g[:, :, 0, :], g[:, :, 1, :], ALU.min)
-            nc.vector.tensor_tensor(hi[:], g[:, :, 0, :], g[:, :, 1, :], ALU.max)
-            nc.vector.tensor_tensor(mn[:], lo[:, :, 0], lo[:, :, 1], ALU.min)
-            nc.vector.tensor_tensor(mx[:], hi[:, :, 0], hi[:, :, 1], ALU.max)
-            nc.vector.tensor_tensor(a[:], y_ps[t][:], mn[:], ALU.max)
-            nc.vector.scalar_tensor_tensor(b_all[:, t, :], mx[:], -0.5, a[:], ALU.mult, ALU.add)
-
-        combine(0)
-        w3_g = sb("w3_g", [P, 2048], BF16)
-        cast_plain(nc.vector.tensor_copy, w3_g, w3_raw, 0, 128)
-        w3_q = quantize("w3", w3_g[:], 512)
-        combine(1)
-        w4_g = sb("w4_g", [P, 2048], BF16)
-        cast_plain(nc.vector.tensor_copy, w4_g, w4_raw, 0, 128)
-        w4_q = quantize("w4", w4_g[:], 512)
-        combine(2)
-        combine(3)
-
-        def woven(ap):
-            return ap.rearrange("p t (c i) -> p c t i", i=4)
-
-        z_g = sb("z_g", [P, S * PACK], BF16)
-        nc.vector.tensor_tensor(
-            z_g[:].rearrange("p (c i t) -> p c t i", i=4, t=PACK),
-            woven(b_all[:]),
-            gn_t[:].unsqueeze(1).unsqueeze(3).broadcast_to([P, S // 4, PACK, 4]),
-            ALU.mult,
-        )
-        z_codes, z_plane = quantize("z", z_g[:], S)
+        z_core = sb("z_core", [P, PACK, S], F32)
+        nc.vector.scalar_tensor_tensor(z_core[:], mx[:], -0.5, upper[:], ALU.mult, ALU.add)
+        z_rounded = sb("z_rounded", [P, PACK * S], BF16)
+        gn_spread = gn_t[:].unsqueeze(1).unsqueeze(3).broadcast_to([P, HALF, PACK, 2])
+        nc.vector.tensor_tensor(woven(z_rounded[:]), by_pairs(z_core[:]), gn_spread, ALU.mult)
+        w4_early_mx = quantize("w4_early", w4_early_rounded)
+        z_mx = quantize("z", z_rounded)
         h_ps = [psum.tile([P, S], F32, name="h_ps%d" % m, tag="yh%d" % m) for m in range(PACK)]
         for m in range(PACK):
-            product(h_ps[m][:], w3_q, slice(P * m, P * (m + 1)), (z_codes[:], z_plane[:]), True, False)
+            product(h_ps[m], w3_mx, m, z_mx, True, False)
 
-        pair = sb("pair", [P, PACK, S], F32)
+        d_gd = sb("d_gd", [P, PACK, S], F32)
         for t in range(PACK):
-            nc.vector.tensor_tensor(pair[:, t, :], d_ps[t][:], gd_got[:, t, :], ALU.mult)
-        z2_g = sb("z2_g", [P, S * PACK], BF16)
-        z2_codes = sb("z2_codes", [P, S], U32)
+            nc.vector.tensor_tensor(d_gd[:, t, :], d_ps[t][:], gd_got[:, t, :], ALU.mult)
+        z2_rounded = sb("z2_rounded", [P, PACK * S], BF16)
+        z2_words = sb("z2_words", [P, S], U32)
         z2_plane = sb("z2_plane", [P, S], U8)
-        for u in range(2):
-            cols = slice(HALF * u, HALF * (u + 1))
-            part = z2_g[:, PACK * HALF * u : PACK * HALF * (u + 1)]
-            nc.vector.tensor_tensor(
-                part.rearrange("p (c i t) -> p c t i", i=4, t=PACK),
-                woven(pair[:, :, cols]), woven(th_got[:, :, cols]), ALU.mult,
-            )
-            nc.vector.quantize_mx(out=z2_codes[:, cols].bitcast(FP8X4), scales=z2_plane[:, cols], in_=part)
-        for m in range(PACK):
-            product(h_ps[m][:], w4_q, slice(P * m, P * (m + 1)), (z2_codes[:], z2_plane[:]), False, True)
+        for c0, c1 in HALVES:
+            part = z2_rounded[:, PACK * c0 : PACK * c1]
+            nc.vector.tensor_tensor(woven(part), by_pairs(d_gd[:, :, c0:c1]), by_pairs(th_got[:, :, c0:c1]), ALU.mult)
+            nc.vector.quantize_mx(out=z2_words[:, c0:c1].bitcast(FP8X4), scales=z2_plane[:, c0:c1], in_=part)
+        for m in range(EARLY_BLOCKS):
+            product(h_ps[m], w4_early_mx, m, (z2_words, z2_plane), False, True)
+        w4_late_mx = quantize("w4_late", w4_late_rounded, reuse="z2_rounded")
+        for m in range(EARLY_BLOCKS, PACK):
+            product(h_ps[m], w4_late_mx, m - EARLY_BLOCKS, (z2_words, z2_plane), False, True)
 
+        h_got = [sb("h_got%d" % m, [P, S], F32) for m in range(PACK)]
+        st_got = [sb("st_got%d" % m, [P, S], F32) for m in range(PACK)]
+        result = [sb("result%d" % m, [P, S], F32) for m in range(PACK)]
+        pieces = [(m, 0, S) for m in range(PACK - 1)] + [(PACK - 1, c0, c1) for c0, c1 in HALVES]
+
+        nc.vector.tensor_copy(h_win[0][:, :S], h_ps[0][:])
+        for m in range(1, PACK):
+            nc.scalar.copy(h_win[m][:, :S], h_ps[m][:])
         for m in range(PACK):
-            h_win = sb("h_win%d" % m, [P, S], F32)
-            h_got = sb("h_got%d" % m, [P, S], F32)
-            st_win = sb("st_win%d" % m, [P, S], F32)
-            st_got = sb("st_got%d" % m, [P, S], F32)
-            res = sb("res%d" % m, [P, S], F32)
-            nc.scalar.copy(h_win[:], h_ps[m][:])
-            for u in range(2):
-                nc.vector.tensor_copy(h_got[:, HALF * u : HALF * (u + 1)], h_win[:].indirect(half(n4_t, u)))
-            nc.vector.tensor_tensor(st_win[:], h_win[:], h_got[:], ALU.max)
-            for u in range(2):
-                nc.scalar.activation(st_got[:, HALF * u : HALF * (u + 1)], st_win[:].indirect(half(n5_t, u)), ACT.Copy)
-            nc.vector.scalar_tensor_tensor(res[:], h_win[:], -0.5, st_got[:], ALU.mult, ALU.add)
-            nc.sync.dma_start(out[P * m : P * (m + 1), :], res[:])
+            if m == N4_ON_SCALAR:
+                nc.scalar.activation(h_got[m][:], h_win[m][:].indirect(n4_t[:]), ACT.Copy)
+            else:
+                nc.vector.tensor_copy(h_got[m][:], h_win[m][:].indirect(n4_t[:]))
+            nc.vector.tensor_tensor(st_win[m][:, :S], h_ps[m][:], h_got[m][:], ALU.max)
+        for m, c0, c1 in pieces:
+            nc.scalar.activation(st_got[m][:, c0:c1], st_win[m][:].indirect(entries(n5_t, c0, c1)), ACT.Copy)
+        for m, c0, c1 in pieces:
+            nc.vector.scalar_tensor_tensor(
+                result[m][:, c0:c1], h_ps[m][:, c0:c1], -0.5, st_got[m][:, c0:c1], ALU.mult, ALU.add
+            )
+            nc.sync.dma_start(out[P * m : P * (m + 1), c0:c1], result[m][:, c0:c1])

@@ -25,7 +25,7 @@ GD_WINDOW = 2 * S
 H_WINDOW = S + HALF
 ST_WINDOW = S + 16
 
-W1_ON_VECTOR = 80
+W1_ON_VECTOR = 56
 EARLY_BLOCKS = 2
 N4_ON_SCALAR = 2
 
@@ -109,20 +109,20 @@ def tile_picked_hjoingmidcubehopb_none_p_kernel(
         offs_t = load_list("offs_t", offs)
         hz_t = load_list("hz_t", hz)
         w1_raw = load_weight("w1_raw", w1)
-        x_tile = sb("x_tile", [P, T], I32)
-        nc.sync.dma_start(x_tile[:], x_words[0].rearrange("p n j -> p (n j)").bitcast(I32))
-        n1_t = load_list("n1_t", n1)
         scale_rows = x_scales[0].bitcast(I32)
         nc.sync.dma_start(x_bytes[0:P:8, :].bitcast(I32), scale_rows)
         for r in range(1, 4):
             nc.sync.dma_start(x_bytes[r:P:32, :].bitcast(I32), scale_rows[r:16:4, :])
+        x_tile = sb("x_tile", [P, T], I32)
+        nc.sync.dma_start(x_tile[:], x_words[0].rearrange("p n j -> p (n j)").bitcast(I32))
+        n1_t = load_list("n1_t", n1)
         w2_raw = load_weight("w2_raw", w2)
+        n2_t = load_list("n2_t", n2)
+        n3_t = load_list("n3_t", n3)
         w3_raw = load_weight("w3_raw", w3)
         w4_raw = load_weight("w4_raw", w4)
         gm_t = load_gain("gm_t", gm)
         gn_t = load_gain("gn_t", gn)
-        n2_t = load_list("n2_t", n2)
-        n3_t = load_list("n3_t", n3)
         n4_t = load_list("n4_t", n4)
         n5_t = load_list("n5_t", n5)
 

from contextlib import ExitStack

import concourse.mybir as mybir

K, T, S, N, H, W = 512, 2048, 256, 512, 512, 1024
FLOPS = 2 * S * (K * H + K * H + H * N + H * N)

F32 = mybir.dt.float32
BF16 = mybir.dt.bfloat16
I32 = mybir.dt.int32
U32 = mybir.dt.uint32
U16 = mybir.dt.uint16
U8 = mybir.dt.uint8
FP8X4 = mybir.dt.float8_e4m3fn_x4
ALU = mybir.AluOpType
ACT = mybir.ActivationFunctionType

P = 128
PACK = 4
HALF = S // 2
HALVES = ((0, HALF), (HALF, S))

Y_WINDOW = W + 16
GD_WINDOW = 2 * S
H_WINDOW = S + HALF
ST_WINDOW = S + 16

W1_ON_VECTOR = 56
EARLY_BLOCKS = 2
N4_ON_SCALAR = 2


def tile_picked_hjoingmidcubehopb_none_p_kernel(
    tc, x_words, x_scales, w1, w2, gn, gm, w3, w4, offs, hz, n1, n2, n3, n4, n5, out
):
    nc = tc.nc
    with ExitStack() as ctx:
        keep = ctx.enter_context(tc.tile_pool(name="keep", bufs=1))
        psum = ctx.enter_context(tc.psum_pool(name="psum", bufs=1))

        def sb(name, shape, dtype, reuse=None):
            return keep.tile(shape, dtype, name=name, tag=reuse or name, align_bytes=64)

        def load_list(name, src):
            tile = keep.tile(list(src.shape), U16, name=name)
            nc.sync.dma_start(tile[:], src)
            return tile

        def load_weight(name, src):
            raw = sb(name, [P, PACK, src.shape[1]], F32)
            nc.sync.dma_start(raw[:], src.rearrange("(p j) c -> p j c", j=PACK))
            return raw

        def load_gain(name, src):
            tile = sb(name, [P, PACK], F32)
            nc.sync.dma_start(tile[:], src.rearrange("(p t) o -> p (t o)", t=PACK))
            return tile

        def entries(lst, c0, c1):
            return lst[:, c0 // 16 : c1 // 16]

        def round_dealt(copy, rounded, raw, m0, m1):
            dst = rounded[:].rearrange("p (t m j) -> p m j t", t=PACK, j=PACK)
            src = raw[:].rearrange("p j (m t) -> p m j t", t=PACK)
            copy(dst[:, m0:m1], src[:, m0:m1])

        def round_plain(copy, rounded, raw, c0, c1):
            dst = rounded[:].rearrange("p (c i j) -> p c j i", i=4, j=PACK)
            copy(dst, raw[:, :, c0:c1].rearrange("p j (c i) -> p c j i", i=4))

        def quantize(name, rounded, reuse=None):
            width = rounded.shape[1] // PACK
            words = sb(name + "_words", [P, width], U32, reuse)
            plane = sb(name + "_plane", [P, width], U8)
            nc.vector.quantize_mx(out=words[:].bitcast(FP8X4), scales=plane[:], in_=rounded[:])
            return words, plane

        def product(acc, weight, block, moving, start, stop):
            cols = slice(P * block, P * (block + 1))
            nc.tensor.matmul_mx(
                out=acc[:],
                lhsT=weight[0][:, cols].bitcast(FP8X4),
                lhsT_scale=weight[1][:, cols],
                rhs=moving[0][:].bitcast(FP8X4),
                rhs_scale=moving[1][:],
                start=start,
                stop=stop,
            )

        def by_pairs(planes):
            return planes.rearrange("p t (c i) -> p c t i", i=2)

        def woven(rounded):
            return rounded.rearrange("p (c i t) -> p c t i", i=2, t=PACK)

        x_bytes = sb("x_bytes", [P, T], U8)
        nc.gpsimd.memset(x_bytes[:].bitcast(I32), 0)
        hz_plane = sb("hz_plane", [P, S], U8)
        nc.gpsimd.memset(hz_plane[:].bitcast(I32), 0)
        y_win = [sb("y_win%d" % t, [P, Y_WINDOW], F32) for t in range(PACK)]
        for win in y_win:
            nc.vector.memset(win[:, S:], 0.0)
        gd_win = [sb("gd_win%d" % t, [P, GD_WINDOW], F32) for t in range(PACK)]
        h_win = [sb("h_win%d" % m, [P, H_WINDOW], F32) for m in range(PACK)]
        st_win = [sb("st_win%d" % m, [P, ST_WINDOW], F32) for m in range(PACK)]
        for win in gd_win + h_win + st_win:
            nc.gpsimd.memset(win[:, S:], 0.0)

        offs_t = load_list("offs_t", offs)
        hz_t = load_list("hz_t", hz)
        w1_raw = load_weight("w1_raw", w1)
        scale_rows = x_scales[0].bitcast(I32)
        nc.sync.dma_start(x_bytes[0:P:8, :].bitcast(I32), scale_rows)
        for r in range(1, 4):
            nc.sync.dma_start(x_bytes[r:P:32, :].bitcast(I32), scale_rows[r:16:4, :])
        x_tile = sb("x_tile", [P, T], I32)
        nc.sync.dma_start(x_tile[:], x_words[0].rearrange("p n j -> p (n j)").bitcast(I32))
        n1_t = load_list("n1_t", n1)
        w2_raw = load_weight("w2_raw", w2)
        n2_t = load_list("n2_t", n2)
        n3_t = load_list("n3_t", n3)
        w3_raw = load_weight("w3_raw", w3)
        w4_raw = load_weight("w4_raw", w4)
        gm_t = load_gain("gm_t", gm)
        gn_t = load_gain("gn_t", gn)
        n4_t = load_list("n4_t", n4)
        n5_t = load_list("n5_t", n5)

        w1_rounded = sb("w1_rounded", [P, PACK * H], BF16)
        round_dealt(nc.vector.tensor_copy, w1_rounded, w1_raw, 0, W1_ON_VECTOR)
        round_dealt(nc.scalar.copy, w1_rounded, w1_raw, W1_ON_VECTOR, P)
        offs_plane = sb("offs_plane", [P, S], U8)
        nc.vector.tensor_copy(offs_plane[:], x_bytes[:].indirect(offs_t[:]))
        w1_mx = quantize("w1", w1_rounded)
        offs_words = sb("offs_words", [P, S], U32)
        nc.vector.tensor_copy(offs_words[:], x_tile[:].bitcast(U32).indirect(offs_t[:]))
        y_ps = [psum.tile([P, S], F32, name="y_ps%d" % t, tag="yh%d" % t) for t in range(PACK)]
        for t in range(PACK):
            product(y_ps[t], w1_mx, t, (offs_words, offs_plane), True, True)
        members = [sb("members%d" % t, [P, W], F32) for t in range(PACK)]
        nc.scalar.copy(y_win[0][:, :S], y_ps[0][:])
        for t in range(PACK):
            if t + 1 < PACK:
                nc.scalar.copy(y_win[t + 1][:, :S], y_ps[t + 1][:])
            nc.scalar.activation(members[t][:], y_win[t][:].indirect(n1_t[:]), ACT.Copy)

        hz_bytes = sb("hz_bytes", [P, S], U8)
        nc.vector.tensor_copy(hz_bytes[:], x_bytes[:].indirect(hz_t[:]))
        for r in range(4):
            nc.sync.dma_start(hz_plane[r:P:32, :].bitcast(I32), hz_bytes[8 * r : P : 32, :].bitcast(I32))
        hz_words = sb("hz_words", [P, S], U32)
        nc.vector.tensor_copy(hz_words[:], x_tile[:].bitcast(U32).indirect(hz_t[:]))
        w2_rounded = sb("w2_rounded", [P, PACK * H], BF16)
        round_dealt(nc.vector.tensor_copy, w2_rounded, w2_raw, 0, P)
        w2_mx = quantize("w2", w2_rounded)
        d_ps = [psum.tile([P, S], F32, name="d_ps%d" % t, tag="d%d" % t) for t in range(PACK)]
        for t in range(PACK):
            product(d_ps[t], w2_mx, t, (hz_words, hz_plane), True, True)

        upper = sb("upper", [P, PACK, S], F32)
        mx = sb("mx", [P, PACK, S], F32)

        def extremes(t):
            four = members[t][:].rearrange("p (j u e) -> p j u e", u=2, e=2)
            left = sb("left%d" % t, [P, 2, S, 2], F32, reuse="w3_raw")
            low, high = left[:, 0], left[:, 1]
            mn = sb("mn%d" % t, [P, S], F32)
            nc.vector.tensor_tensor(low, four[:, :, 0, :], four[:, :, 1, :], ALU.min)
            nc.vector.tensor_tensor(high, four[:, :, 0, :], four[:, :, 1, :], ALU.max)
            nc.vector.tensor_tensor(mn[:], low[:, :, 0], low[:, :, 1], ALU.min)
            nc.vector.tensor_tensor(mx[:, t, :], high[:, :, 0], high[:, :, 1], ALU.max)
            nc.vector.tensor_tensor(upper[:, t, :], y_ps[t][:], mn[:], ALU.max)

        w3_rounded = sb("w3_rounded", [P, PACK * N], BF16)
        round_plain(nc.vector.tensor_copy, w3_rounded, w3_raw, 0, N)
        extremes(0)
        w3_mx = quantize("w3", w3_rounded)
        extremes(1)

        th_win = [sb("th_win%d" % t, [P, S], F32) for t in range(PACK)]
        for t in range(PACK):
            nc.scalar.activation(gd_win[t][:, :S], d_ps[t][:], ACT.Copy, scale=gm_t[:, t : t + 1])
            nc.scalar.activation(th_win[t][:], d_ps[t][:], ACT.Tanh)
        gd_got = sb("gd_got", [P, PACK, S], F32)
        th_got = sb("th_got", [P, PACK, S], F32)
        for t in range(PACK):
            nc.scalar.activation(gd_got[:, t, :], gd_win[t][:].indirect(n2_t[:]), ACT.Copy)
        for c0, c1 in HALVES:
            for t in range(PACK):
                nc.scalar.activation(th_got[:, t, c0:c1], th_win[t][:].indirect(entries(n3_t, c0, c1)), ACT.Copy)

        early_columns = P * EARLY_BLOCKS
        w4_early_rounded = sb("w4_early_rounded", [P, PACK * early_columns], BF16)
        round_plain(nc.vector.tensor_copy, w4_early_rounded, w4_raw, 0, early_columns)
        w4_late_rounded = sb("w4_late_rounded", [P, PACK * (N - early_columns)], BF16, reuse="th_win%d" % (PACK - 1))
        round_plain(nc.scalar.copy, w4_late_rounded, w4_raw, early_columns, N)
        extremes(2)
        extremes(3)

        z_core = sb("z_core", [P, PACK, S], F32)
        nc.vector.scalar_tensor_tensor(z_core[:], mx[:], -0.5, upper[:], ALU.mult, ALU.add)
        z_rounded = sb("z_rounded", [P, PACK * S], BF16)
        gn_spread = gn_t[:].unsqueeze(1).unsqueeze(3).broadcast_to([P, HALF, PACK, 2])
        nc.vector.tensor_tensor(woven(z_rounded[:]), by_pairs(z_core[:]), gn_spread, ALU.mult)
        w4_early_mx = quantize("w4_early", w4_early_rounded)
        z_mx = quantize("z", z_rounded)
        h_ps = [psum.tile([P, S], F32, name="h_ps%d" % m, tag="yh%d" % m) for m in range(PACK)]
        for m in range(PACK):
            product(h_ps[m], w3_mx, m, z_mx, True, False)

        d_gd = sb("d_gd", [P, PACK, S], F32)
        for t in range(PACK):
            nc.vector.tensor_tensor(d_gd[:, t, :], d_ps[t][:], gd_got[:, t, :], ALU.mult)
        z2_rounded = sb("z2_rounded", [P, PACK * S], BF16)
        z2_words = sb("z2_words", [P, S], U32)
        z2_plane = sb("z2_plane", [P, S], U8)
        for c0, c1 in HALVES:
            part = z2_rounded[:, PACK * c0 : PACK * c1]
            nc.vector.tensor_tensor(woven(part), by_pairs(d_gd[:, :, c0:c1]), by_pairs(th_got[:, :, c0:c1]), ALU.mult)
            nc.vector.quantize_mx(out=z2_words[:, c0:c1].bitcast(FP8X4), scales=z2_plane[:, c0:c1], in_=part)
        for m in range(EARLY_BLOCKS):
            product(h_ps[m], w4_early_mx, m, (z2_words, z2_plane), False, True)
        w4_late_mx = quantize("w4_late", w4_late_rounded, reuse="z2_rounded")
        for m in range(EARLY_BLOCKS, PACK):
            product(h_ps[m], w4_late_mx, m - EARLY_BLOCKS, (z2_words, z2_plane), False, True)

        h_got = [sb("h_got%d" % m, [P, S], F32) for m in range(PACK)]
        st_got = [sb("st_got%d" % m, [P, S], F32) for m in range(PACK)]
        result = [sb("result%d" % m, [P, S], F32) for m in range(PACK)]
        pieces = [(m, 0, S) for m in range(PACK - 1)] + [(PACK - 1, c0, c1) for c0, c1 in HALVES]

        nc.vector.tensor_copy(h_win[0][:, :S], h_ps[0][:])
        for m in range(1, PACK):
            nc.scalar.copy(h_win[m][:, :S], h_ps[m][:])
        for m in range(PACK):
            if m == N4_ON_SCALAR:
                nc.scalar.activation(h_got[m][:], h_win[m][:].indirect(n4_t[:]), ACT.Copy)
            else:
                nc.vector.tensor_copy(h_got[m][:], h_win[m][:].indirect(n4_t[:]))
            nc.vector.tensor_tensor(st_win[m][:, :S], h_ps[m][:], h_got[m][:], ALU.max)
        for m, c0, c1 in pieces:
            nc.scalar.activation(st_got[m][:, c0:c1], st_win[m][:].indirect(entries(n5_t, c0, c1)), ACT.Copy)
        for m, c0, c1 in pieces:
            nc.vector.scalar_tensor_tensor(
                result[m][:, c0:c1], h_ps[m][:, c0:c1], -0.5, st_got[m][:, c0:c1], ALU.mult, ALU.add
            )
            nc.sync.dma_start(out[P * m : P * (m + 1), c0:c1], result[m][:, c0:c1])
